import numpy as np, ml_dtypes
CORES = [65,66,69,71,193,194,197,199,321,322,325,327,449,450,453,455]
N = 16
F = 32
def setup_inputs(rng):
    x = (rng.standard_normal((N, 128, 128), dtype=np.float32) / 11).astype(ml_dtypes.bfloat16)
    w = rng.standard_normal((128, F), dtype=np.float32).astype(ml_dtypes.bfloat16)
    return {"x": x, "xt": x.transpose(0, 2, 1).copy(), "w": np.broadcast_to(w, (N, 128, F)).copy()}
def setup_inputs_big(rng):
    d = setup_inputs(rng)
    for k in ("x", "xt", "w"): d[k] = (d[k].astype(np.float32) * 1024.0).astype(d[k].dtype)
    return d
def setup_inputs_small(rng):
    d = setup_inputs(rng)
    for k in ("x", "xt", "w"): d[k] = (d[k].astype(np.float32) * (1 / 1024.0)).astype(d[k].dtype)
    return d
def setup_inputs_apart(rng):
    d = setup_inputs(rng)
    f = (10.0 ** rng.permutation(np.linspace(-1.5, 1.5, N))).astype(np.float32).reshape(N, 1, 1)
    for k in ("x", "xt"): d[k] = (d[k].astype(np.float32) * f).astype(d[k].dtype)
    return d
def tie_inputs(x):
    x = dict(x)
    x["xt"] = x["x"].transpose(0, 2, 1).copy(); x["w"] = np.broadcast_to(x["w"][0], x["w"].shape).copy()
    return x
def reference(x, xt, w):
    X, XT, W = x.astype(np.float64), xt.astype(np.float64), w.astype(np.float64)
    s = sum(X[j].T @ (XT[j].T @ W[j]) for j in range(N)).astype(ml_dtypes.bfloat16 if x.dtype != np.float64 else np.float64)
    return {"y": np.broadcast_to(s, (N,) + s.shape)}

@@ -1,0 +1,117 @@
+from concourse.bass import DstId, RemoteDMATransfer
+from concourse.mybir import AluOpType
+
+F = 32
+
+SCRATCH = {
+    "xs": ("sbuf", [128, 128], "bfloat16"),
+    "ws": ("sbuf", [128, F], "bfloat16"),
+    "gb": ("sbuf", [128, 128], "bfloat16"),
+    "pb": ("sbuf", [128, F], "bfloat16"),
+    "l1": ("sbuf", [128, 3 * F], "bfloat16"),
+    "qb": ("sbuf", [128, F], "bfloat16"),
+    "l2": ("sbuf", [128, 3 * F], "bfloat16"),
+    "a1": ("sbuf", [128, F], "float32"),
+    "a2": ("sbuf", [128, F], "float32"),
+    "b1": ("sbuf", [128, F], "float32"),
+    "b2": ("sbuf", [128, F], "float32"),
+    "yb": ("sbuf", [128, F], "bfloat16"),
+    "gp": ("psum", [128, 512], "float32"),
+    "pp": ("psum", [128, 512], "float32"),
+}
+SEMAPHORES = ["sx", "sw", "sg", "sgb", "sp", "spb", "c1", "o1", "sv", "sq", "c2", "o2", "sy", "st", "ls"]
+
+
+def _bits(m):
+    return [b for b in range(m.bit_length()) if (m >> b) & 1]
+
+
+def _mask(bs):
+    m = 0
+    for b in bs:
+        m |= 1 << b
+    return m
+
+
+def _ranks_of_host(T, topo, h):
+    return sorted(d for d in T.cores if topo.host(d) == h)
+
+
+def _twin(T, topo, d, h):
+    return _ranks_of_host(T, topo, h)[_ranks_of_host(T, topo, topo.host(d)).index(d)]
+
+
+def _plan(core, T, topo):
+    me = topo.host(core)
+    chipm = [d for d in _ranks_of_host(T, topo, me) if topo.chip(d) == topo.chip(core)]
+    same = [d for d in chipm if topo.die(d) == topo.die(core)]
+    other = [d for d in chipm if topo.die(d) != topo.die(core)]
+    near = [d for d in same if d != core][0]
+    far = other[same.index(core)]
+    hosts = sorted({topo.host(d) for d in T.cores})
+    rack_h = [h for h in hosts if h != me and topo.rack(h) == topo.rack(me)][0]
+    cable_h = [h for h in hosts if topo.rack(h) != topo.rack(me) and topo.may_write(core, _twin(T, topo, core, h))][0]
+    return (near, rack_h), (far, cable_h)
+
+
+def _gather(g, core, T, topo, partner, host, src, land, sem_chip, sem_off):
+    t1, t2 = _twin(T, topo, core, host), _twin(T, topo, partner, host)
+    off = [b for b in _bits(topo.mask(core, t1)) if b in _bits(topo.mask(core, t2))]
+    on = [b for b in _bits(topo.mask(core, partner)) if b not in off]
+    half = len(off) // 2
+    jobs = [(partner, 0, on[:half], sem_chip), (t1, 1, off[:half], sem_off), (t2, 2, off[half:2 * half], sem_off)]
+    trs = []
+    for d, slot, eng, sem in jobs:
+        rid, pid = topo.addr(d, core)
+        trs.append(RemoteDMATransfer(dst_ids=[DstId(rid=rid, pnc=pid)], dma_engine_mask=_mask(eng), remote_sem=sem,
+                                     src=src[:], dst=land[:, slot * F:(slot + 1) * F]))
+    g.remote_dma_fused(trs, local_sem=T.sem.ls)
+    return half, 2 * half
+
+
+def rank_program(g, core, T, topo):
+    if T.rank_of(core) is None:
+        return
+    S, add = T.sem, AluOpType.add
+    te, ve = g.tensor, g.vector
+    (p1, h1), (p2, h2) = _plan(core, T, topo)
+
+    g.sync.dma_start(T.xs[:], T.x[:]).then_inc(S.sx, 16)
+    g.scalar.dma_start(T.ws[:], T.w[:]).then_inc(S.sw, 16)
+
+    te.wait_ge(S.sx, 16)
+    te.matmul(T.gp[:, 0:128], T.xs[:], T.xs[:], True, True).then_inc(S.sg, 1)
+    te.wait_ge(S.sw, 16)
+    te.wait_ge(S.sgb, 1)
+    te.matmul(T.pp[:, 0:F], T.gb[:], T.ws[:], True, True).then_inc(S.sp, 1)
+
+    ve.wait_ge(S.sg, 1)
+    ve.tensor_copy(T.gb[:], T.gp[:, 0:128]).then_inc(S.sgb, 1)
+    ve.wait_ge(S.sp, 1)
+    ve.tensor_copy(T.pb[:], T.pp[:, 0:F]).then_inc(S.spb, 1)
+
+    g.wait_ge(S.spb, 1)
+    nc, no = _gather(g, core, T, topo, p1, h1, T.pb, T.l1, S.c1, S.o1)
+    ve.wait_ge(S.c1, nc)
+    ve.tensor_tensor(T.a1[:], T.pp[:, 0:F], T.l1[:, 0:F], add).then_inc(S.sv, 1)
+    ve.wait_ge(S.o1, no)
+    ve.wait_ge(S.sv, 1)
+    ve.tensor_tensor(T.a2[:], T.a1[:], T.l1[:, F:2 * F], add).then_inc(S.sv, 1)
+    ve.wait_ge(S.sv, 2)
+    ve.tensor_tensor(T.qb[:], T.a2[:], T.l1[:, 2 * F:3 * F], add).then_inc(S.sq, 1)
+
+    g.wait_ge(S.sq, 1)
+    _gather(g, core, T, topo, p2, h2, T.qb, T.l2, S.c2, S.o2)
+    ve.wait_ge(S.sq, 1)
+    ve.wait_ge(S.c2, nc)
+    ve.tensor_tensor(T.b1[:], T.qb[:], T.l2[:, 0:F], add).then_inc(S.sv, 1)
+    ve.wait_ge(S.o2, no)
+    ve.wait_ge(S.sv, 3)
+    ve.tensor_tensor(T.b2[:], T.b1[:], T.l2[:, F:2 * F], add).then_inc(S.sv, 1)
+    ve.wait_ge(S.sv, 4)
+    ve.tensor_tensor(T.yb[:], T.b2[:], T.l2[:, 2 * F:3 * F], add).then_inc(S.sy, 1)
+
+    g.sync.wait_ge(S.sy, 1)
+    g.sync.dma_start(T.y[:], T.yb[:]).then_inc(S.st, 16)
+    g.wait_ge(S.ls, 2 * (nc + no))
+    g.wait_ge(S.st, 16)

@@ -5,21 +5,25 @@ F = 32
 
 SCRATCH = {
     "xs": ("sbuf", [128, 128], "bfloat16"),
+    "xp": ("sbuf", [128, 128], "bfloat16"),
     "ws": ("sbuf", [128, F], "bfloat16"),
     "gb": ("sbuf", [128, 128], "bfloat16"),
+    "g2": ("sbuf", [128, 128], "bfloat16"),
     "pb": ("sbuf", [128, F], "bfloat16"),
-    "l1": ("sbuf", [128, 3 * F], "bfloat16"),
+    "l1": ("sbuf", [128, 2 * F], "bfloat16"),
     "qb": ("sbuf", [128, F], "bfloat16"),
     "l2": ("sbuf", [128, 3 * F], "bfloat16"),
-    "a1": ("sbuf", [128, F], "float32"),
     "a2": ("sbuf", [128, F], "float32"),
     "b1": ("sbuf", [128, F], "float32"),
     "b2": ("sbuf", [128, F], "float32"),
     "yb": ("sbuf", [128, F], "bfloat16"),
     "gp": ("psum", [128, 512], "float32"),
     "pp": ("psum", [128, 512], "float32"),
+    "gq": ("psum", [128, 512], "float32"),
+    "pq": ("psum", [128, 512], "float32"),
 }
-SEMAPHORES = ["sx", "sw", "sg", "sgb", "sp", "spb", "c1", "o1", "sv", "sq", "c2", "o2", "sy", "st", "ls"]
+SEMAPHORES = ["sx", "sw", "sg", "sgb", "sp", "spb", "cx", "sh", "sg2", "spq", "o1", "sv", "sq", "c2", "o2", "sy", "st",
+              "ls"]
 
 
 def _bits(m):
@@ -54,19 +58,17 @@ def _plan(core, T, topo):
     return (near, rack_h), (far, cable_h)
 
 
-def _gather(g, core, T, topo, partner, host, src, land, sem_chip, sem_off):
+def _engines(core, T, topo, partner, host):
     t1, t2 = _twin(T, topo, core, host), _twin(T, topo, partner, host)
     off = [b for b in _bits(topo.mask(core, t1)) if b in _bits(topo.mask(core, t2))]
     on = [b for b in _bits(topo.mask(core, partner)) if b not in off]
-    half = len(off) // 2
-    jobs = [(partner, 0, on[:half], sem_chip), (t1, 1, off[:half], sem_off), (t2, 2, off[half:2 * half], sem_off)]
-    trs = []
-    for d, slot, eng, sem in jobs:
-        rid, pid = topo.addr(d, core)
-        trs.append(RemoteDMATransfer(dst_ids=[DstId(rid=rid, pnc=pid)], dma_engine_mask=_mask(eng), remote_sem=sem,
-                                     src=src[:], dst=land[:, slot * F:(slot + 1) * F]))
-    g.remote_dma_fused(trs, local_sem=T.sem.ls)
-    return half, 2 * half
+    return off, on
+
+
+def _tr(core, topo, d, eng, sem, src, dst):
+    rid, pid = topo.addr(d, core)
+    return RemoteDMATransfer(dst_ids=[DstId(rid=rid, pnc=pid)], dma_engine_mask=_mask(eng), remote_sem=sem,
+                             src=src, dst=dst)
 
 
 def rank_program(g, core, T, topo):
@@ -75,43 +77,62 @@ def rank_program(g, core, T, topo):
     S, add = T.sem, AluOpType.add
     te, ve = g.tensor, g.vector
     (p1, h1), (p2, h2) = _plan(core, T, topo)
+    off1, on1 = _engines(core, T, topo, p1, h1)
+    off2, on2 = _engines(core, T, topo, p2, h2)
+    k1, k2 = len(off1) // 2, len(off2) // 2
 
     g.sync.dma_start(T.xs[:], T.x[:]).then_inc(S.sx, 16)
     g.scalar.dma_start(T.ws[:], T.w[:]).then_inc(S.sw, 16)
+
+    g.wait_ge(S.sx, 16)
+    rid, pid = topo.addr(p1, core)
+    g.remote_dma(T.xp[:], T.xs[:], S.cx, S.ls, pid, rid, _mask(on1))
 
     te.wait_ge(S.sx, 16)
     te.matmul(T.gp[:, 0:128], T.xs[:], T.xs[:], True, True).then_inc(S.sg, 1)
     te.wait_ge(S.sw, 16)
     te.wait_ge(S.sgb, 1)
     te.matmul(T.pp[:, 0:F], T.gb[:], T.ws[:], True, True).then_inc(S.sp, 1)
+    te.matmul(T.pq[:, 0:F], T.gb[:], T.ws[:], True, False)
+    te.wait_ge(S.cx, len(on1))
+    te.matmul(T.gq[:, 0:128], T.xp[:], T.xp[:], True, True).then_inc(S.sh, 1)
+    te.wait_ge(S.sg2, 1)
+    te.matmul(T.pq[:, 0:F], T.g2[:], T.ws[:], False, True).then_inc(S.spq, 1)
 
     ve.wait_ge(S.sg, 1)
     ve.tensor_copy(T.gb[:], T.gp[:, 0:128]).then_inc(S.sgb, 1)
     ve.wait_ge(S.sp, 1)
     ve.tensor_copy(T.pb[:], T.pp[:, 0:F]).then_inc(S.spb, 1)
+    ve.wait_ge(S.sh, 1)
+    ve.tensor_copy(T.g2[:], T.gq[:, 0:128]).then_inc(S.sg2, 1)
 
     g.wait_ge(S.spb, 1)
-    nc, no = _gather(g, core, T, topo, p1, h1, T.pb, T.l1, S.c1, S.o1)
-    ve.wait_ge(S.c1, nc)
-    ve.tensor_tensor(T.a1[:], T.pp[:, 0:F], T.l1[:, 0:F], add).then_inc(S.sv, 1)
-    ve.wait_ge(S.o1, no)
+    g.remote_dma_fused([
+        _tr(core, topo, _twin(T, topo, core, h1), off1[:k1], S.o1, T.pb[:], T.l1[:, 0:F]),
+        _tr(core, topo, _twin(T, topo, p1, h1), off1[k1:2 * k1], S.o1, T.pb[:], T.l1[:, F:2 * F]),
+    ], local_sem=S.ls)
+    ve.wait_ge(S.spq, 1)
+    ve.wait_ge(S.o1, 2 * k1)
+    ve.tensor_tensor(T.a2[:], T.pq[:, 0:F], T.l1[:, 0:F], add).then_inc(S.sv, 1)
     ve.wait_ge(S.sv, 1)
-    ve.tensor_tensor(T.a2[:], T.a1[:], T.l1[:, F:2 * F], add).then_inc(S.sv, 1)
-    ve.wait_ge(S.sv, 2)
-    ve.tensor_tensor(T.qb[:], T.a2[:], T.l1[:, 2 * F:3 * F], add).then_inc(S.sq, 1)
+    ve.tensor_tensor(T.qb[:], T.a2[:], T.l1[:, F:2 * F], add).then_inc(S.sq, 1)
 
     g.wait_ge(S.sq, 1)
-    _gather(g, core, T, topo, p2, h2, T.qb, T.l2, S.c2, S.o2)
+    g.remote_dma_fused([
+        _tr(core, topo, p2, on2, S.c2, T.qb[:], T.l2[:, 0:F]),
+        _tr(core, topo, _twin(T, topo, core, h2), off2[:k2], S.o2, T.qb[:], T.l2[:, F:2 * F]),
+        _tr(core, topo, _twin(T, topo, p2, h2), off2[k2:2 * k2], S.o2, T.qb[:], T.l2[:, 2 * F:3 * F]),
+    ], local_sem=S.ls)
     ve.wait_ge(S.sq, 1)
-    ve.wait_ge(S.c2, nc)
+    ve.wait_ge(S.c2, len(on2))
     ve.tensor_tensor(T.b1[:], T.qb[:], T.l2[:, 0:F], add).then_inc(S.sv, 1)
-    ve.wait_ge(S.o2, no)
-    ve.wait_ge(S.sv, 3)
+    ve.wait_ge(S.o2, 2 * k2)
+    ve.wait_ge(S.sv, 2)
     ve.tensor_tensor(T.b2[:], T.b1[:], T.l2[:, F:2 * F], add).then_inc(S.sv, 1)
-    ve.wait_ge(S.sv, 4)
+    ve.wait_ge(S.sv, 3)
     ve.tensor_tensor(T.yb[:], T.b2[:], T.l2[:, 2 * F:3 * F], add).then_inc(S.sy, 1)
 
     g.sync.wait_ge(S.sy, 1)
     g.sync.dma_start(T.y[:], T.yb[:]).then_inc(S.st, 16)
-    g.wait_ge(S.ls, 2 * (nc + no))
+    g.wait_ge(S.ls, len(on1) + 2 * k1 + len(on2) + 2 * k2)
     g.wait_ge(S.st, 16)

@@ -22,8 +22,8 @@ SCRATCH = {
     "gq": ("psum", [128, 512], "float32"),
     "pq": ("psum", [128, 512], "float32"),
 }
-SEMAPHORES = ["sx", "sw", "sg", "sgb", "sp", "spb", "cx", "sh", "sg2", "spq", "o1", "sv", "sq", "c2", "o2", "sy", "st",
-              "ls"]
+SEMAPHORES = ["sx", "sw", "sg", "sgb", "sp", "spb", "cx", "sh", "sg2", "spq", "o1", "u1", "sv", "sq", "c2", "o2", "u2",
+              "sy", "st", "ls"]
 
 
 def _bits(m):
@@ -71,6 +71,11 @@ def _tr(core, topo, d, eng, sem, src, dst):
                              src=src, dst=dst)
 
 
+def _send(g, core, topo, d, eng, rsem, lsem, src, dst):
+    rid, pid = topo.addr(d, core)
+    g.remote_dma(dst, src, rsem, lsem, pid, rid, _mask(eng))
+
+
 def rank_program(g, core, T, topo):
     if T.rank_of(core) is None:
         return
@@ -79,14 +84,12 @@ def rank_program(g, core, T, topo):
     (p1, h1), (p2, h2) = _plan(core, T, topo)
     off1, on1 = _engines(core, T, topo, p1, h1)
     off2, on2 = _engines(core, T, topo, p2, h2)
-    k1, k2 = len(off1) // 2, len(off2) // 2
 
     g.sync.dma_start(T.xs[:], T.x[:]).then_inc(S.sx, 16)
     g.scalar.dma_start(T.ws[:], T.w[:]).then_inc(S.sw, 16)
 
     g.wait_ge(S.sx, 16)
-    rid, pid = topo.addr(p1, core)
-    g.remote_dma(T.xp[:], T.xs[:], S.cx, S.ls, pid, rid, _mask(on1))
+    _send(g, core, topo, p1, on1, S.cx, S.ls, T.xs[:], T.xp[:])
 
     te.wait_ge(S.sx, 16)
     te.matmul(T.gp[:, 0:128], T.xs[:], T.xs[:], True, True).then_inc(S.sg, 1)
@@ -107,32 +110,32 @@ def rank_program(g, core, T, topo):
     ve.tensor_copy(T.g2[:], T.gq[:, 0:128]).then_inc(S.sg2, 1)
 
     g.wait_ge(S.spb, 1)
-    g.remote_dma_fused([
-        _tr(core, topo, _twin(T, topo, core, h1), off1[:k1], S.o1, T.pb[:], T.l1[:, 0:F]),
-        _tr(core, topo, _twin(T, topo, p1, h1), off1[k1:2 * k1], S.o1, T.pb[:], T.l1[:, F:2 * F]),
-    ], local_sem=S.ls)
+    _send(g, core, topo, _twin(T, topo, core, h1), off1, S.o1, S.ls, T.pb[:], T.l1[:, 0:F])
+    _send(g, core, topo, _twin(T, topo, p1, h1), off1, S.u1, S.ls, T.pb[:], T.l1[:, F:2 * F])
     ve.wait_ge(S.spq, 1)
-    ve.wait_ge(S.o1, 2 * k1)
+    ve.wait_ge(S.o1, len(off1))
     ve.tensor_tensor(T.a2[:], T.pq[:, 0:F], T.l1[:, 0:F], add).then_inc(S.sv, 1)
+    ve.wait_ge(S.u1, len(off1))
     ve.wait_ge(S.sv, 1)
     ve.tensor_tensor(T.qb[:], T.a2[:], T.l1[:, F:2 * F], add).then_inc(S.sq, 1)
 
     g.wait_ge(S.sq, 1)
     g.remote_dma_fused([
         _tr(core, topo, p2, on2, S.c2, T.qb[:], T.l2[:, 0:F]),
-        _tr(core, topo, _twin(T, topo, core, h2), off2[:k2], S.o2, T.qb[:], T.l2[:, F:2 * F]),
-        _tr(core, topo, _twin(T, topo, p2, h2), off2[k2:2 * k2], S.o2, T.qb[:], T.l2[:, 2 * F:3 * F]),
+        _tr(core, topo, _twin(T, topo, core, h2), off2, S.o2, T.qb[:], T.l2[:, F:2 * F]),
     ], local_sem=S.ls)
+    _send(g, core, topo, _twin(T, topo, p2, h2), off2, S.u2, S.ls, T.qb[:], T.l2[:, 2 * F:3 * F])
     ve.wait_ge(S.sq, 1)
     ve.wait_ge(S.c2, len(on2))
     ve.tensor_tensor(T.b1[:], T.qb[:], T.l2[:, 0:F], add).then_inc(S.sv, 1)
-    ve.wait_ge(S.o2, 2 * k2)
+    ve.wait_ge(S.o2, len(off2))
     ve.wait_ge(S.sv, 2)
     ve.tensor_tensor(T.b2[:], T.b1[:], T.l2[:, F:2 * F], add).then_inc(S.sv, 1)
+    ve.wait_ge(S.u2, len(off2))
     ve.wait_ge(S.sv, 3)
     ve.tensor_tensor(T.yb[:], T.b2[:], T.l2[:, 2 * F:3 * F], add).then_inc(S.sy, 1)
 
     g.sync.wait_ge(S.sy, 1)
     g.sync.dma_start(T.y[:], T.yb[:]).then_inc(S.st, 16)
-    g.wait_ge(S.ls, len(on1) + 2 * k1 + len(on2) + 2 * k2)
+    g.wait_ge(S.ls, len(on1) + 2 * len(off1) + len(on2) + 2 * len(off2))
     g.wait_ge(S.st, 16)

from concourse.bass import DstId, RemoteDMATransfer
from concourse.mybir import AluOpType

F = 32

SCRATCH = {
    "xs": ("sbuf", [128, 128], "bfloat16"),
    "xp": ("sbuf", [128, 128], "bfloat16"),
    "ws": ("sbuf", [128, F], "bfloat16"),
    "gb": ("sbuf", [128, 128], "bfloat16"),
    "g2": ("sbuf", [128, 128], "bfloat16"),
    "pb": ("sbuf", [128, F], "bfloat16"),
    "l1": ("sbuf", [128, 2 * F], "bfloat16"),
    "qb": ("sbuf", [128, F], "bfloat16"),
    "l2": ("sbuf", [128, 3 * F], "bfloat16"),
    "a2": ("sbuf", [128, F], "float32"),
    "b1": ("sbuf", [128, F], "float32"),
    "b2": ("sbuf", [128, F], "float32"),
    "yb": ("sbuf", [128, F], "bfloat16"),
    "gp": ("psum", [128, 512], "float32"),
    "pp": ("psum", [128, 512], "float32"),
    "gq": ("psum", [128, 512], "float32"),
    "pq": ("psum", [128, 512], "float32"),
}
SEMAPHORES = ["sx", "sw", "sg", "sgb", "sp", "spb", "cx", "sh", "sg2", "spq", "o1", "u1", "sv", "sq", "c2", "o2", "u2",
              "sy", "st", "ls"]


def _bits(m):
    return [b for b in range(m.bit_length()) if (m >> b) & 1]


def _mask(bs):
    m = 0
    for b in bs:
        m |= 1 << b
    return m


def _ranks_of_host(T, topo, h):
    return sorted(d for d in T.cores if topo.host(d) == h)


def _twin(T, topo, d, h):
    return _ranks_of_host(T, topo, h)[_ranks_of_host(T, topo, topo.host(d)).index(d)]


def _plan(core, T, topo):
    me = topo.host(core)
    chipm = [d for d in _ranks_of_host(T, topo, me) if topo.chip(d) == topo.chip(core)]
    same = [d for d in chipm if topo.die(d) == topo.die(core)]
    other = [d for d in chipm if topo.die(d) != topo.die(core)]
    near = [d for d in same if d != core][0]
    far = other[same.index(core)]
    hosts = sorted({topo.host(d) for d in T.cores})
    rack_h = [h for h in hosts if h != me and topo.rack(h) == topo.rack(me)][0]
    cable_h = [h for h in hosts if topo.rack(h) != topo.rack(me) and topo.may_write(core, _twin(T, topo, core, h))][0]
    return (near, rack_h), (far, cable_h)


def _engines(core, T, topo, partner, host):
    t1, t2 = _twin(T, topo, core, host), _twin(T, topo, partner, host)
    off = [b for b in _bits(topo.mask(core, t1)) if b in _bits(topo.mask(core, t2))]
    on = [b for b in _bits(topo.mask(core, partner)) if b not in off]
    return off, on


def _tr(core, topo, d, eng, sem, src, dst):
    rid, pid = topo.addr(d, core)
    return RemoteDMATransfer(dst_ids=[DstId(rid=rid, pnc=pid)], dma_engine_mask=_mask(eng), remote_sem=sem,
                             src=src, dst=dst)


def _send(g, core, topo, d, eng, rsem, lsem, src, dst):
    rid, pid = topo.addr(d, core)
    g.remote_dma(dst, src, rsem, lsem, pid, rid, _mask(eng))


def rank_program(g, core, T, topo):
    if T.rank_of(core) is None:
        return
    S, add = T.sem, AluOpType.add
    te, ve = g.tensor, g.vector
    (p1, h1), (p2, h2) = _plan(core, T, topo)
    off1, on1 = _engines(core, T, topo, p1, h1)
    off2, on2 = _engines(core, T, topo, p2, h2)

    g.sync.dma_start(T.xs[:], T.x[:]).then_inc(S.sx, 16)
    g.scalar.dma_start(T.ws[:], T.w[:]).then_inc(S.sw, 16)

    g.wait_ge(S.sx, 16)
    _send(g, core, topo, p1, on1, S.cx, S.ls, T.xs[:], T.xp[:])

    te.wait_ge(S.sx, 16)
    te.matmul(T.gp[:, 0:128], T.xs[:], T.xs[:], True, True).then_inc(S.sg, 1)
    te.wait_ge(S.sw, 16)
    te.wait_ge(S.sgb, 1)
    te.matmul(T.pp[:, 0:F], T.gb[:], T.ws[:], True, True).then_inc(S.sp, 1)
    te.matmul(T.pq[:, 0:F], T.gb[:], T.ws[:], True, False)
    te.wait_ge(S.cx, len(on1))
    te.matmul(T.gq[:, 0:128], T.xp[:], T.xp[:], True, True).then_inc(S.sh, 1)
    te.wait_ge(S.sg2, 1)
    te.matmul(T.pq[:, 0:F], T.g2[:], T.ws[:], False, True).then_inc(S.spq, 1)

    ve.wait_ge(S.sg, 1)
    ve.tensor_copy(T.gb[:], T.gp[:, 0:128]).then_inc(S.sgb, 1)
    ve.wait_ge(S.sp, 1)
    ve.tensor_copy(T.pb[:], T.pp[:, 0:F]).then_inc(S.spb, 1)
    ve.wait_ge(S.sh, 1)
    ve.tensor_copy(T.g2[:], T.gq[:, 0:128]).then_inc(S.sg2, 1)

    g.wait_ge(S.spb, 1)
    _send(g, core, topo, _twin(T, topo, core, h1), off1, S.o1, S.ls, T.pb[:], T.l1[:, 0:F])
    _send(g, core, topo, _twin(T, topo, p1, h1), off1, S.u1, S.ls, T.pb[:], T.l1[:, F:2 * F])
    ve.wait_ge(S.spq, 1)
    ve.wait_ge(S.o1, len(off1))
    ve.tensor_tensor(T.a2[:], T.pq[:, 0:F], T.l1[:, 0:F], add).then_inc(S.sv, 1)
    ve.wait_ge(S.u1, len(off1))
    ve.wait_ge(S.sv, 1)
    ve.tensor_tensor(T.qb[:], T.a2[:], T.l1[:, F:2 * F], add).then_inc(S.sq, 1)

    g.wait_ge(S.sq, 1)
    g.remote_dma_fused([
        _tr(core, topo, p2, on2, S.c2, T.qb[:], T.l2[:, 0:F]),
        _tr(core, topo, _twin(T, topo, core, h2), off2, S.o2, T.qb[:], T.l2[:, F:2 * F]),
    ], local_sem=S.ls)
    _send(g, core, topo, _twin(T, topo, p2, h2), off2, S.u2, S.ls, T.qb[:], T.l2[:, 2 * F:3 * F])
    ve.wait_ge(S.sq, 1)
    ve.wait_ge(S.c2, len(on2))
    ve.tensor_tensor(T.b1[:], T.qb[:], T.l2[:, 0:F], add).then_inc(S.sv, 1)
    ve.wait_ge(S.o2, len(off2))
    ve.wait_ge(S.sv, 2)
    ve.tensor_tensor(T.b2[:], T.b1[:], T.l2[:, F:2 * F], add).then_inc(S.sv, 1)
    ve.wait_ge(S.u2, len(off2))
    ve.wait_ge(S.sv, 3)
    ve.tensor_tensor(T.yb[:], T.b2[:], T.l2[:, 2 * F:3 * F], add).then_inc(S.sy, 1)

    g.sync.wait_ge(S.sy, 1)
    g.sync.dma_start(T.y[:], T.yb[:]).then_inc(S.st, 16)
    g.wait_ge(S.ls, len(on1) + 2 * len(off1) + len(on2) + 2 * len(off2))
    g.wait_ge(S.st, 16)
